import numpy as np
import ml_dtypes


def mxq(x, axis, fmt="e4m3"):
    dtype, down = {"e4m3": (ml_dtypes.float8_e4m3fn, 7), "e5m2": (ml_dtypes.float8_e5m2, 14)}[fmt]
    v = np.moveaxis(np.asarray(x, np.float32).astype(ml_dtypes.bfloat16).astype(np.float64), axis, -1)
    blocks = v.reshape(v.shape[:-1] + (-1, 32))
    amax = np.abs(blocks).max(-1, keepdims=True)
    byte = np.maximum(np.where(amax > 0, np.frexp(amax)[1] - 1 + 127, 0) - down, 1)
    scale = np.exp2(byte - 127.0)
    codes = (blocks / scale).astype(np.float32).astype(dtype).astype(np.float64)
    return np.moveaxis((codes * scale).reshape(v.shape), -1, axis)


WIDE = False


def mx_kscale(k):
    if not WIDE:
        return np.ones(k)
    levels = np.array([10, -10, 5, -5, 0])
    if k % 512:
        return np.exp2(np.random.permutation(np.resize(levels, k // 32))).repeat(32)
    a = np.empty((k // 512, 16))
    for p in range(k // 512):
        a[p, :8] = np.random.permutation(np.resize(levels, 8))
        for g in range(8):
            far = levels[np.abs(levels - a[p, g]) >= 10]
            a[p, g + 8] = far[np.random.randint(len(far))]
    return np.exp2(a.ravel()).repeat(32)


def f64(x):
    return np.asarray(x).astype(np.float64)


def striped(idx):
    return np.tile(idx.reshape(-1, 16).T, (8, 1)).astype(np.uint16)


def unstriped(offs):
    return offs[:16].T.reshape(-1).astype(np.int64)


E2M1 = np.array([0.0, 0.5, 1.0, 1.5, 2.0, 3.0, 4.0, 6.0, -0.0, -0.5, -1.0, -1.5, -2.0, -3.0, -4.0, -6.0])


def pack_weight(w, fmt):
    k, n = w.shape
    w = f64(np.asarray(w, np.float32).astype(ml_dtypes.bfloat16)).reshape(k // 32, 32, n)
    amax = np.abs(w).max(1)
    if fmt == "e4m3":
        byte = np.frexp(amax)[1] - 1 + 127 - 7
    else:
        mant, ex = np.frexp(amax / 6.0)
        byte = np.where(mant > 0.5, ex, ex - 1) + 127
    byte = np.clip(np.where(amax > 0, byte, 1), 1, 254)
    scaled = (w * np.exp2(127.0 - byte)[:, None, :]).reshape(k, n).astype(np.float32)
    by_word = np.ascontiguousarray(scaled.reshape(k // 512, 128, 4, n).transpose(0, 1, 3, 2))
    if fmt == "e4m3":
        words = by_word.astype(ml_dtypes.float8_e4m3fn).view(np.uint8)
    else:
        c = by_word.astype(ml_dtypes.float4_e2m1fn).view(np.uint8) & 0xF
        words = (c[..., 0::2] | (c[..., 1::2] << 4)).reshape(k // 512, 128, 2 * n)
    return np.ascontiguousarray(words), np.ascontiguousarray(byte.astype(np.uint8).reshape(k // 512, 16, n))


def unpack_weight(words, scales, fmt):
    g, _, n = scales.shape
    words = np.ascontiguousarray(words).reshape(g, 128, n, -1)
    if fmt == "e4m3":
        vals = words.view(ml_dtypes.float8_e4m3fn).astype(np.float64)
    else:
        nib = np.empty((g, 128, n, 4), np.uint8)
        nib[..., 0::2] = words & 0xF
        nib[..., 1::2] = words >> 4
        vals = E2M1[nib]
    vals = vals * np.repeat(np.exp2(scales.astype(np.float64) - 127.0), 8, axis=1)[..., None]
    return vals.transpose(0, 1, 3, 2).reshape(g * 512, n)


def gelu(v):
    return 0.5 * v * (1.0 + np.tanh(np.sqrt(2.0 / np.pi) * (v + 0.044715 * v**3)))


def striped8(idx):
    return np.concatenate([v.reshape(-1, 16).T for v in idx]).astype(np.uint16)


def unstriped8(offs):
    return np.stack([offs[16 * g:16 * g + 16].T.reshape(-1) for g in range(8)]).astype(np.int64)


def runs(v, idx8):
    k = np.arange(v.shape[0])
    return v[k[:, None], idx8[k % 512 // 64]]


def bf(x):
    return np.asarray(x, np.float32).astype(ml_dtypes.bfloat16)


def planes(Y):
    n, m = Y.shape
    b = f64(bf(Y)).reshape(n // 32, 32, m)
    amax = np.abs(b).max(1)
    byte = np.clip(np.where(amax > 0, np.frexp(amax)[1] - 1 + 127 - 7, 1), 1, 254)
    codes = (b * np.exp2(127.0 - byte)[:, None, :]).reshape(n, m).astype(np.float32).astype(ml_dtypes.float8_e4m3fn).view(np.uint8)
    words = codes.reshape(n // 512, 128, 4, m).transpose(0, 1, 3, 2)
    return np.ascontiguousarray(words), np.ascontiguousarray(byte.astype(np.uint8).reshape(n // 512, 16, m))


T, S, P, K, H, N = 2048, 1024, 512, 1536, 1024, 512


def setup_inputs():
    n = np.random.standard_normal
    s = mx_kscale(K)[:, None]
    u = mx_kscale(H)[:, None]
    d = {}
    d["tab_words"], d["tab_scales"] = pack_weight(n((K, T)) * s, "e4m3")
    d["offs"] = striped8(np.stack([np.random.permutation(T)[:S] for _ in range(8)]))
    d["pos1"] = striped(np.random.permutation(S)[:P])
    d["pos2"] = striped(np.random.permutation(S)[:P])
    d["w1"] = (1.4 * n((K, H)) / K**0.5 / s).astype(np.float32)
    d["b1"] = (0.6 * n(H)).astype(np.float32)
    d["gain"] = (np.exp(0.3 * n(H)) * u[:, 0]).astype(np.float32)
    w4 = n((H, N)) * np.exp(0.8 * n(N)) / H**0.5 / u
    d["w4_words"], d["w4_scales"] = pack_weight(w4, "e2m1")
    d["w3"] = (n((H, N)) / H**0.5 / u).astype(np.float32)
    return d


def reference(tab_words, tab_scales, offs, pos1, pos2, w1, b1, gain, w4_words, w4_scales, w3):
    v = runs(unpack_weight(tab_words, tab_scales, "e4m3"), unstriped8(offs))
    h = (mxq(f64(w1), 0, "e4m3").T @ v) + f64(b1)[:, None]
    z = (h[:, unstriped(pos1)] - np.tanh(h[:, unstriped(pos2)])) * f64(gain)[:, None]
    zq = mxq(z, 0, "e4m3")
    change = unpack_weight(w4_words, w4_scales, "e2m1").T @ zq
    extent = mxq(f64(w3), 0, "e4m3").T @ zq
    y = change / (1.0 + np.abs(extent))
    words, scales = planes(y)
    return y, words, scales

@@ -1,0 +1,331 @@
+from contextlib import ExitStack
+
+import concourse.mybir as mybir
+
+T, S, M, K, H, N = 2048, 1024, 512, 1536, 1024, 512
+FLOPS = 2 * K * H * S + 2 * 2 * H * N * M
+
+F32 = mybir.dt.float32
+BF16 = mybir.dt.bfloat16
+I32 = mybir.dt.int32
+U32 = mybir.dt.uint32
+U16 = mybir.dt.uint16
+U8 = mybir.dt.uint8
+FP8X4 = mybir.dt.float8_e4m3fn_x4
+FP4X4 = mybir.dt.float4_e2m1fn_x4
+ACT = mybir.ActivationFunctionType
+ALU = mybir.AluOpType
+
+P = 128
+PACK = 4
+PASS = P * PACK
+BANK = 512
+BLOCK = 128
+PLANE_ROW = (0, 8, 4)
+CHUNKS = ((0, 128), (128, 128), (256, 128), (384, 128))
+
+
+def tile_list_song_theme_features_kernel(
+    tc, tab_words, tab_scales, offs, pos1, pos2, w1, b1, gain, w4_words, w4_scales, w3, out_0, out_1, out_2
+):
+    nc = tc.nc
+    with ExitStack() as ctx:
+        keep = ctx.enter_context(tc.tile_pool(name="keep", bufs=1))
+        ring = ctx.enter_context(tc.tile_pool(name="ring", bufs=1))
+        shared = ctx.enter_context(tc.tile_pool(name="shared", bufs=1))
+        psum = ctx.enter_context(tc.psum_pool(name="psum", bufs=8))
+
+        offs_sb = keep.tile([P, S // 16], U16, name="offs_sb")
+        pos1_sb = keep.tile([P, M // 16], U16, name="pos1_sb")
+        pos2_sb = keep.tile([P, M // 16], U16, name="pos2_sb")
+        b1_sb = keep.tile([P, 2, PACK], F32, name="b1_sb")
+        gain_sb = keep.tile([P, 2, PACK], F32, name="gain_sb")
+
+        def big(kib, shape, dtype, name):
+            return shared.tile(shape, dtype, name=name, offset=1024 * kib, align_bytes=64)
+
+        tab_sb = [big(0, [P, T], I32, "tab0"), big(14, [P, T], I32, "tab1")]
+        v_words = [keep.tile([P, S], I32, name="v_words%d" % a, align_bytes=64) for a in range(3)]
+        tab_sc = keep.tile([P, T], U8, name="tab_sc", align_bytes=64)
+        picked_sc = keep.tile([P, S], U8, name="picked_sc", align_bytes=64)
+        v_sc = keep.tile([P, S], U8, name="v_sc", align_bytes=64)
+        w4_raw = keep.tile([P, 2 * 2 * N], U8, name="w4_raw", align_bytes=64)
+        w4s_raw = keep.tile([P, 2 * N], U8, name="w4s_raw", align_bytes=64)
+        y_words = keep.tile([P, M], I32, name="y_words", align_bytes=64)
+        y_sc = keep.tile([P, M], U8, name="y_sc", align_bytes=64)
+        warm = keep.tile([P, 1], F32, name="warm")
+
+        def quant_tiles(name, width):
+            words = keep.tile([P, width], I32, name=name + "_w", align_bytes=64)
+            scales = keep.tile([P, width], U8, name=name + "_s", align_bytes=64)
+            return words, scales
+
+        w1q = {(a, b): quant_tiles("w1q%d%d" % (a, b), 512) for a in range(3) for b in range(2)}
+        w3q = [quant_tiles("w3q%d" % b, 512) for b in range(2)]
+        zq = [quant_tiles("zq%d" % b, 512) for b in range(2)]
+
+        tab32 = tab_words.rearrange("a p t i -> a p (t i)").bitcast(I32)
+        tsc32 = tab_scales.bitcast(I32)
+        w4s32 = w4_scales.bitcast(I32)
+        tab_sc32 = tab_sc[:].bitcast(I32)
+        w4s_raw32 = w4s_raw[:].bitcast(I32)
+
+        def load_rows(name, kib, src):
+            raw = big(kib, [P, PACK, src.shape[1]], F32, name)
+            nc.sync.dma_start(out=raw[:], in_=src.rearrange("(p j) c -> p j c", j=PACK))
+            return raw
+
+        def stage_tile():
+            return ring.tile([P, 2048], BF16, name="stage", tag="stage", bufs=4, align_bytes=64)
+
+        def cast(engine, stage, src, q0, q1):
+            dst = stage[:].rearrange("p (t q j) -> p q j t", t=PACK, j=PACK)[:, q0:q1]
+            src = src.rearrange("p j (q t) -> p q j t", t=PACK)
+            if engine == "scalar":
+                nc.scalar.activation(out=dst, in_=src, func=ACT.Copy)
+            else:
+                nc.vector.tensor_copy(out=dst, in_=src)
+
+        def quantize(q, stage, c0, c1, base=0):
+            nc.vector.quantize_mx(
+                out=q[0][:, c0:c1].bitcast(FP8X4), scales=q[1][:, c0:c1], in_=stage[:, PACK * (c0 - base) : PACK * (c1 - base)]
+            )
+
+        nc.vector.memset(tab_sc32, 0)
+        nc.vector.memset(w4s_raw32, 0)
+        nc.sync.dma_start(offs_sb[:], offs)
+        nc.sync.dma_start(pos2_sb[:], pos2)
+        nc.sync.dma_start(pos1_sb[:], pos1)
+        nc.sync.dma_start(out=tab_sb[0][:], in_=tab32[0])
+        nc.sync.dma_start(out=tab_sb[1][:], in_=tab32[1])
+        raw_w1 = {}
+        raw_w1[0, 0] = load_rows("w1_00", 24, w1[0:512, 0:512])
+        for e in range(2):
+            nc.sync.dma_start(out=tab_sc32[e:P:8, :], in_=tsc32[0:2, e:16:2, :].rearrange("a g w -> g a w"))
+            nc.sync.dma_start(out=tab_sc32[4 + e : P : 16, :], in_=tsc32[2, e:16:2, :])
+        nc.gpsimd.dma_start(out=b1_sb[:], in_=b1.rearrange("(b p t) -> p b t", b=2, t=PACK))
+        nc.gpsimd.dma_start(
+            out=w4_raw[:].bitcast(I32).rearrange("p (a w) -> p a w", a=2), in_=w4_words.bitcast(I32).rearrange("a p w -> p a w")
+        )
+        for r in range(4):
+            nc.gpsimd.dma_start(
+                out=w4s_raw32[r:P:32, :].rearrange("p (a w) -> p a w", a=2), in_=w4s32[:, r:16:4, :].rearrange("a q w -> q a w")
+            )
+        nc.gpsimd.dma_start(out=gain_sb[:], in_=gain.rearrange("(b p t) -> p b t", b=2, t=PACK))
+
+        def pick_words(a):
+            nc.vector.tensor_copy(v_words[a][:].bitcast(U32), tab_sb[a][:].bitcast(U32).indirect(offs_sb[:]))
+
+        pick_words(0)
+        tab_sb.append(big(0, [P, T], I32, "tab2"))
+        nc.sync.dma_start(out=tab_sb[2][:], in_=tab32[2])
+        pick_words(1)
+        raw_w1[1, 0] = load_rows("w1_10", 16, w1[512:1024, 0:512])
+        raw_w2a = load_rows("w1_20a", 12, w1[1024:1536, 0:256])
+        nc.vector.tensor_copy(picked_sc[:], tab_sc[:].indirect(offs_sb[:]))
+        picked32 = picked_sc[:].bitcast(I32)
+        v_sc32 = v_sc[:].bitcast(I32)
+        nc.vector.tensor_copy(out=v_sc32, in_=picked32)
+        for e in range(2):
+            nc.scalar.dma_start(out=v_sc32[2 + e : 114 + e : 4, :], in_=picked32[16 + e : P : 4, :])
+
+        def h_pass(banks, a, b, t):
+            for hf in range(2):
+                cols = slice(hf * BANK, (hf + 1) * BANK)
+                nc.tensor.matmul_mx(
+                    out=banks[t][hf][:],
+                    lhsT=w1q[a, b][0][:, t * P : (t + 1) * P].bitcast(FP8X4),
+                    lhsT_scale=w1q[a, b][1][:, t * P : (t + 1) * P],
+                    rhs=v_words[a][:, cols].bitcast(FP8X4),
+                    rhs_scale=v_sc[PLANE_ROW[a] : P, cols],
+                    start=(a == 0),
+                    stop=(a == 2),
+                )
+
+        def new_banks():
+            return [[psum.tile([P, BANK], F32, name="acc", tag="acc") for hf in range(2)] for t in range(PACK)]
+
+        banks0 = new_banks()
+        st = stage_tile()
+        cast("scalar", st, raw_w1[0, 0][:], 0, 128)
+        raw_w2b = load_rows("w1_20b", 24, w1[1024:1536, 256:512])
+        quantize(w1q[0, 0], st, 0, 512)
+        pick_words(2)
+        raw_w1[0, 1] = load_rows("w1_01", 0, w1[0:512, 512:1024])
+        st = stage_tile()
+        cast("scalar", st, raw_w1[1, 0][:, :, 0:256], 0, 64)
+        cast("vector", st, raw_w1[1, 0][:, :, 256:512], 64, 128)
+        raw_w1[1, 1] = load_rows("w1_11", 16, w1[512:1024, 512:1024])
+        st2 = big(40, [P, 2048], BF16, "stage_w1_20")
+        cast("scalar", st2, raw_w2a[:], 0, 64)
+        quantize(w1q[1, 0], st, 0, 512)
+        cast("scalar", st2, raw_w2b[:, :, 0:128], 64, 96)
+        cast("vector", st2, raw_w2b[:, :, 128:256], 96, 128)
+        raw_w1[2, 1] = load_rows("w1_21", 24, w1[1024:1536, 512:1024])
+        raw_w3 = [load_rows("w3_0", 8, w3[0:512, :])]
+        for t in range(PACK):
+            quantize(w1q[2, 0], st2, t * P, (t + 1) * P)
+            for a in range(3):
+                h_pass(banks0, a, 0, t)
+
+        w4_sb = big(40, [P, 2 * 2 * N], U8, "w4_sb")
+        w4_sc = big(42, [P, 2 * N], U8, "w4_sc")
+        nc.vector.tensor_copy(
+            out=w4_sb[:].bitcast(U16).rearrange("p (a t q) -> p a q t", a=2, t=PACK),
+            in_=w4_raw[:].bitcast(U16).rearrange("p (a q t) -> p a q t", a=2, t=PACK),
+        )
+        nc.vector.tensor_copy(
+            out=w4_sc[:].rearrange("p (a t q) -> p a q t", a=2, t=PACK),
+            in_=w4s_raw[:].rearrange("p (a q t) -> p a q t", a=2, t=PACK),
+        )
+
+        def evacuate(banks, b, t):
+            h = ring.tile([P, S], F32, name="h", tag="h", bufs=6)
+            for hf in range(2):
+                dst = h[:, hf * BANK : (hf + 1) * BANK]
+                nc.scalar.activation(out=dst, in_=banks[t][hf][:], func=ACT.Identity, bias=b1_sb[:, b, t : t + 1])
+            return h
+
+        def pick2(h, b, t):
+            g = big(32 + 2 * t, [P, M], F32, "g2_%d%d" % (b, t))
+            nc.vector.tensor_copy(g[:], h[:].indirect(pos2_sb[:]))
+            return g
+
+        def tanh(g):
+            th = ring.tile([P, M], F32, name="th", tag="th", bufs=6)
+            nc.scalar.activation(out=th[:], in_=g[:], func=ACT.Tanh)
+            return th
+
+        def pick1(d, h, th, m0, w):
+            nc.vector.tensor_tensor(d, h[:].indirect(pos1_sb[:, m0 // 16 : (m0 + w) // 16]), th[:, m0 : m0 + w], ALU.subtract)
+
+        def scale_round(stage, d, b, w):
+            nc.vector.tensor_tensor(
+                out=stage[:, 0 : PACK * w].rearrange("p (c i t) -> p c t i", i=4, t=PACK),
+                in0=d[:].rearrange("p t (c i) -> p c t i", i=4),
+                in1=gain_sb[:, b, :].unsqueeze(1).unsqueeze(3).to_broadcast([P, w // 4, PACK, 4]),
+                op=ALU.mult,
+            )
+
+        d0 = keep.tile([P, PACK, M], F32, name="d0")
+        h = [None] * PACK
+        g = [None] * PACK
+        th = [None] * PACK
+        h[0] = evacuate(banks0, 0, 0)
+        g[0] = pick2(h[0], 0, 0)
+        for t in range(PACK):
+            if t + 1 < PACK:
+                h[t + 1] = evacuate(banks0, 0, t + 1)
+                g[t + 1] = pick2(h[t + 1], 0, t + 1)
+            if t == PACK - 1:
+                stw = [big(32, [P, 2048], BF16, "stage_w1_01")]
+                cast("scalar", stw[0], raw_w1[0, 1][:], 0, 128)
+                raw_w3.append(load_rows("w3_1", 0, w3[512:1024, :]))
+            th[t] = tanh(g[t])
+            pick1(d0[:, t, :], h[t], th[t], 0, M)
+
+        banks1 = new_banks()
+        quantize(w1q[0, 1], stw[0], 0, 512)
+        st = stage_tile()
+        cast("scalar", st, raw_w1[1, 1][:], 0, 128)
+        quantize(w1q[1, 1], st, 0, 512)
+        st = stage_tile()
+        cast("scalar", st, raw_w1[2, 1][:], 0, 128)
+        stz = stage_tile()
+        scale_round(stz, d0, 0, M)
+        for t in range(PACK):
+            quantize(w1q[2, 1], st, t * P, (t + 1) * P)
+            for a in range(3):
+                h_pass(banks1, a, 1, t)
+        quantize(zq[0], stz, 0, 512)
+        st = stage_tile()
+        cast("scalar", st, raw_w3[0][:, :, 0:256], 0, 64)
+        cast("vector", st, raw_w3[0][:, :, 256:512], 64, 128)
+
+        h[0] = evacuate(banks1, 1, 0)
+        g[0] = pick2(h[0], 1, 0)
+        quantize(w3q[0], st, 0, 512)
+        for t in range(PACK):
+            if t + 1 < PACK:
+                h[t + 1] = evacuate(banks1, 1, t + 1)
+                g[t + 1] = pick2(h[t + 1], 1, t + 1)
+            th[t] = tanh(g[t])
+        st = stage_tile()
+        cast("scalar", st, raw_w3[1][:], 0, 128)
+        nc.scalar.activation(out=warm[:], in_=th[PACK - 1][:, 0:1], func=ACT.Abs_reciprocal_sqrt, bias=2.0)
+
+        y_view = out_0.rearrange("(p t) m -> p t m", t=PACK)
+        words_view = out_1[0].rearrange("p m t -> p (m t)").bitcast(I32)
+
+        def products(m0):
+            cols = slice(m0, m0 + BLOCK)
+            extent = psum.tile([P, PACK, BLOCK], F32, name="acc", tag="acc")
+            change = psum.tile([P, PACK, BLOCK], F32, name="acc", tag="acc")
+            for t in range(PACK):
+                for b in range(2):
+                    nc.tensor.matmul_mx(
+                        out=extent[:, t, :],
+                        lhsT=w3q[b][0][:, t * P : (t + 1) * P].bitcast(FP8X4),
+                        lhsT_scale=w3q[b][1][:, t * P : (t + 1) * P],
+                        rhs=zq[b][0][:, cols].bitcast(FP8X4),
+                        rhs_scale=zq[b][1][:, cols],
+                        start=(b == 0),
+                        stop=(b == 1),
+                    )
+            for t in range(PACK):
+                for b in range(2):
+                    c0 = b * N + t * P
+                    nc.tensor.matmul_mx(
+                        out=change[:, t, :],
+                        lhsT=w4_sb[:, 2 * c0 : 2 * (c0 + P)].bitcast(FP4X4),
+                        lhsT_scale=w4_sc[:, c0 : c0 + P],
+                        rhs=zq[b][0][:, cols].bitcast(FP8X4),
+                        rhs_scale=zq[b][1][:, cols],
+                        start=(b == 0),
+                        stop=(b == 1),
+                    )
+            return extent, change
+
+        def damping(extent):
+            a = ring.tile([P, BANK], F32, name="absx", tag="absx", bufs=2)
+            r = ring.tile([P, BANK], F32, name="root", tag="root", bufs=2)
+            r2 = ring.tile([P, BANK], F32, name="recip", tag="recip", bufs=2)
+            nc.scalar.activation(out=a[:], in_=extent[:].rearrange("p t m -> p (t m)"), func=ACT.Abs)
+            nc.scalar.activation(out=r[:], in_=a[:], func=ACT.Abs_reciprocal_sqrt, bias=1.0)
+            nc.scalar.activation(out=r2[:], in_=r[:], func=ACT.Square)
+            return r2
+
+        def finish(change, r2, m0):
+            y = ring.tile([P, PACK, BLOCK], F32, name="y", tag="y", bufs=4)
+            yb = ring.tile([P, PACK * BLOCK], BF16, name="yb", tag="yb", bufs=2, align_bytes=64)
+            nc.vector.tensor_tensor(
+                out=y[:].rearrange("p t m -> p (t m)"), in0=change[:].rearrange("p t m -> p (t m)"), in1=r2[:], op=ALU.mult
+            )
+            nc.sync.dma_start(out=y_view[:, :, m0 : m0 + BLOCK], in_=y[:])
+            nc.vector.tensor_copy(
+                out=yb[:].rearrange("p (c i t) -> p c t i", i=4, t=PACK), in_=y[:].rearrange("p t (c i) -> p c t i", i=4)
+            )
+            quantize((y_words, y_sc), yb, m0, m0 + BLOCK, base=m0)
+            nc.sync.dma_start(out=words_view[:, m0 : m0 + BLOCK], in_=y_words[:, m0 : m0 + BLOCK])
+
+        pending = []
+        for m0, w in CHUNKS:
+            d = keep.tile([P, PACK, w], F32, name="d1_%d" % m0)
+            for t in range(PACK):
+                pick1(d[:, t, :], h[t], th[t], m0, w)
+            if m0 == 0:
+                quantize(w3q[1], st, 0, 512)
+            stz = stage_tile()
+            scale_round(stz, d, 1, w)
+            quantize(zq[1], stz, m0, m0 + w, base=m0)
+            for mb in range(m0, m0 + w, BLOCK):
+                extent, change = products(mb)
+                pending.append((change, damping(extent), mb))
+        for change, r2, mb in pending:
+            finish(change, r2, mb)
+
+        y_sc32 = y_sc[:].bitcast(I32)
+        sc_view = out_2[0].bitcast(I32)
+        for q in range(4):
+            eng = nc.sync if q % 2 == 0 else nc.scalar
+            eng.dma_start(out=sc_view[4 * q : 4 * q + 4, :], in_=y_sc32[32 * q : 32 * q + 4, :])

@@ -21,8 +21,8 @@ PACK = 4
 PASS = P * PACK
 BANK = 512
 BLOCK = 128
+LINE = 4
 PLANE_ROW = (0, 8, 4)
-CHUNKS = ((0, 128), (128, 128), (256, 128), (384, 128))
 
 
 def tile_list_song_theme_features_kernel(
@@ -35,297 +35,291 @@ def tile_list_song_theme_features_kernel(
         shared = ctx.enter_context(tc.tile_pool(name="shared", bufs=1))
         psum = ctx.enter_context(tc.psum_pool(name="psum", bufs=8))
 
+        def placed(name, kib, shape, dtype):
+            return shared.tile(shape, dtype, name=name, offset=1024 * kib, align_bytes=64)
+
+        def mx_tiles(name, width):
+            words = keep.tile([P, width], I32, name=name + "_words", align_bytes=64)
+            scales = keep.tile([P, width], U8, name=name + "_scales", align_bytes=64)
+            return words, scales
+
+        def load_pass(name, kib, rows):
+            raw = placed(name, kib, [P, PACK, rows.shape[1]], F32)
+            nc.sync.dma_start(out=raw[:], in_=rows.rearrange("(p j) c -> p j c", j=PACK))
+            return raw
+
+        def load_table(a, kib):
+            words = placed("tab%d" % a, kib, [P, T], I32)
+            nc.sync.dma_start(out=words[:], in_=tab_words[a].rearrange("p t i -> p (t i)").bitcast(I32))
+            return words
+
+        def round_weight(engine, rounded, raw, q0):
+            count = raw.shape[2] // PACK
+            dst = rounded[:].rearrange("p (t q j) -> p q j t", t=PACK, j=PACK)[:, q0 : q0 + count]
+            src = raw.rearrange("p j (q t) -> p q j t", t=PACK)
+            if engine is nc.scalar:
+                nc.scalar.activation(out=dst, in_=src, func=ACT.Copy)
+            else:
+                nc.vector.tensor_copy(out=dst, in_=src)
+
+        def round_in_halves(rounded, raw):
+            round_weight(nc.scalar, rounded, raw[:, :, 0 : PASS // 2], 0)
+            round_weight(nc.vector, rounded, raw[:, :, PASS // 2 : PASS], P // 2)
+
+        def quantize(tiles, c0, values):
+            cols = slice(c0, c0 + values.shape[1] // PACK)
+            nc.vector.quantize_mx(out=tiles[0][:, cols].bitcast(FP8X4), scales=tiles[1][:, cols], in_=values)
+
+        def interleaved(tile):
+            return tile.rearrange("p (c i t) -> p c t i", i=LINE, t=PACK)
+
+        def by_slice(tile):
+            return tile.rearrange("p t (c i) -> p c t i", i=LINE)
+
         offs_sb = keep.tile([P, S // 16], U16, name="offs_sb")
         pos1_sb = keep.tile([P, M // 16], U16, name="pos1_sb")
         pos2_sb = keep.tile([P, M // 16], U16, name="pos2_sb")
         b1_sb = keep.tile([P, 2, PACK], F32, name="b1_sb")
         gain_sb = keep.tile([P, 2, PACK], F32, name="gain_sb")
 
-        def big(kib, shape, dtype, name):
-            return shared.tile(shape, dtype, name=name, offset=1024 * kib, align_bytes=64)
-
-        tab_sb = [big(0, [P, T], I32, "tab0"), big(14, [P, T], I32, "tab1")]
-        v_words = [keep.tile([P, S], I32, name="v_words%d" % a, align_bytes=64) for a in range(3)]
-        tab_sc = keep.tile([P, T], U8, name="tab_sc", align_bytes=64)
-        picked_sc = keep.tile([P, S], U8, name="picked_sc", align_bytes=64)
-        v_sc = keep.tile([P, S], U8, name="v_sc", align_bytes=64)
-        w4_raw = keep.tile([P, 2 * 2 * N], U8, name="w4_raw", align_bytes=64)
-        w4s_raw = keep.tile([P, 2 * N], U8, name="w4s_raw", align_bytes=64)
-        y_words = keep.tile([P, M], I32, name="y_words", align_bytes=64)
-        y_sc = keep.tile([P, M], U8, name="y_sc", align_bytes=64)
-        warm = keep.tile([P, 1], F32, name="warm")
-
-        def quant_tiles(name, width):
-            words = keep.tile([P, width], I32, name=name + "_w", align_bytes=64)
-            scales = keep.tile([P, width], U8, name=name + "_s", align_bytes=64)
-            return words, scales
-
-        w1q = {(a, b): quant_tiles("w1q%d%d" % (a, b), 512) for a in range(3) for b in range(2)}
-        w3q = [quant_tiles("w3q%d" % b, 512) for b in range(2)]
-        zq = [quant_tiles("zq%d" % b, 512) for b in range(2)]
-
-        tab32 = tab_words.rearrange("a p t i -> a p (t i)").bitcast(I32)
-        tsc32 = tab_scales.bitcast(I32)
-        w4s32 = w4_scales.bitcast(I32)
+        tab_sc = placed("tab_sc", 31, [P, T], U8)
         tab_sc32 = tab_sc[:].bitcast(I32)
-        w4s_raw32 = w4s_raw[:].bitcast(I32)
-
-        def load_rows(name, kib, src):
-            raw = big(kib, [P, PACK, src.shape[1]], F32, name)
-            nc.sync.dma_start(out=raw[:], in_=src.rearrange("(p j) c -> p j c", j=PACK))
-            return raw
-
-        def stage_tile():
-            return ring.tile([P, 2048], BF16, name="stage", tag="stage", bufs=4, align_bytes=64)
-
-        def cast(engine, stage, src, q0, q1):
-            dst = stage[:].rearrange("p (t q j) -> p q j t", t=PACK, j=PACK)[:, q0:q1]
-            src = src.rearrange("p j (q t) -> p q j t", t=PACK)
-            if engine == "scalar":
-                nc.scalar.activation(out=dst, in_=src, func=ACT.Copy)
-            else:
-                nc.vector.tensor_copy(out=dst, in_=src)
-
-        def quantize(q, stage, c0, c1, base=0):
-            nc.vector.quantize_mx(
-                out=q[0][:, c0:c1].bitcast(FP8X4), scales=q[1][:, c0:c1], in_=stage[:, PACK * (c0 - base) : PACK * (c1 - base)]
-            )
-
         nc.vector.memset(tab_sc32, 0)
-        nc.vector.memset(w4s_raw32, 0)
+        w4_raw = placed("w4_raw", 15, [P, 2 * 2 * N], U8)
+        nc.sync.dma_start(
+            out=w4_raw[:].bitcast(I32).rearrange("p (b w) -> p b w", b=2), in_=w4_words.bitcast(I32).rearrange("b p w -> p b w")
+        )
         nc.sync.dma_start(offs_sb[:], offs)
         nc.sync.dma_start(pos2_sb[:], pos2)
         nc.sync.dma_start(pos1_sb[:], pos1)
-        nc.sync.dma_start(out=tab_sb[0][:], in_=tab32[0])
-        nc.sync.dma_start(out=tab_sb[1][:], in_=tab32[1])
-        raw_w1 = {}
-        raw_w1[0, 0] = load_rows("w1_00", 24, w1[0:512, 0:512])
+        tab0 = load_table(0, 43)
+        rows32 = tab_scales.bitcast(I32)
         for e in range(2):
-            nc.sync.dma_start(out=tab_sc32[e:P:8, :], in_=tsc32[0:2, e:16:2, :].rearrange("a g w -> g a w"))
-            nc.sync.dma_start(out=tab_sc32[4 + e : P : 16, :], in_=tsc32[2, e:16:2, :])
+            nc.sync.dma_start(out=tab_sc32[e:P:8, :], in_=rows32[0:2, e:16:2, :].rearrange("a g w -> g a w"))
+            nc.sync.dma_start(out=tab_sc32[PLANE_ROW[2] + e : P : 16, :], in_=rows32[2, e:16:2, :])
         nc.gpsimd.dma_start(out=b1_sb[:], in_=b1.rearrange("(b p t) -> p b t", b=2, t=PACK))
-        nc.gpsimd.dma_start(
-            out=w4_raw[:].bitcast(I32).rearrange("p (a w) -> p a w", a=2), in_=w4_words.bitcast(I32).rearrange("a p w -> p a w")
-        )
-        for r in range(4):
-            nc.gpsimd.dma_start(
-                out=w4s_raw32[r:P:32, :].rearrange("p (a w) -> p a w", a=2), in_=w4s32[:, r:16:4, :].rearrange("a q w -> q a w")
-            )
         nc.gpsimd.dma_start(out=gain_sb[:], in_=gain.rearrange("(b p t) -> p b t", b=2, t=PACK))
 
-        def pick_words(a):
-            nc.vector.tensor_copy(v_words[a][:].bitcast(U32), tab_sb[a][:].bitcast(U32).indirect(offs_sb[:]))
+        w4_sb = keep.tile([P, 2 * 2 * N], U8, name="w4_sb", align_bytes=64)
+        nc.vector.tensor_copy(
+            out=w4_sb[:].bitcast(U16).rearrange("p (b t q) -> p b q t", b=2, t=PACK),
+            in_=w4_raw[:].bitcast(U16).rearrange("p (b q t) -> p b q t", b=2, t=PACK),
+        )
+        tab1 = load_table(1, 8)
+        w1_raw00 = load_pass("w1_raw00", 16, w1[0:PASS, 0:PASS])
 
-        pick_words(0)
-        tab_sb.append(big(0, [P, T], I32, "tab2"))
-        nc.sync.dma_start(out=tab_sb[2][:], in_=tab32[2])
-        pick_words(1)
-        raw_w1[1, 0] = load_rows("w1_10", 16, w1[512:1024, 0:512])
-        raw_w2a = load_rows("w1_20a", 12, w1[1024:1536, 0:256])
+        picked_sc = keep.tile([P, S], U8, name="picked_sc", align_bytes=64)
         nc.vector.tensor_copy(picked_sc[:], tab_sc[:].indirect(offs_sb[:]))
-        picked32 = picked_sc[:].bitcast(I32)
+        tab2 = load_table(2, 24)
+        v_sc = keep.tile([P, S], U8, name="v_sc", align_bytes=64)
         v_sc32 = v_sc[:].bitcast(I32)
-        nc.vector.tensor_copy(out=v_sc32, in_=picked32)
+        nc.vector.tensor_copy(out=v_sc32, in_=picked_sc[:].bitcast(I32))
         for e in range(2):
-            nc.scalar.dma_start(out=v_sc32[2 + e : 114 + e : 4, :], in_=picked32[16 + e : P : 4, :])
+            nc.sync.dma_start(out=v_sc32[2 + e : P - 14 + e : 4, :], in_=v_sc32[16 + e : P : 4, :])
 
-        def h_pass(banks, a, b, t):
-            for hf in range(2):
-                cols = slice(hf * BANK, (hf + 1) * BANK)
-                nc.tensor.matmul_mx(
-                    out=banks[t][hf][:],
-                    lhsT=w1q[a, b][0][:, t * P : (t + 1) * P].bitcast(FP8X4),
-                    lhsT_scale=w1q[a, b][1][:, t * P : (t + 1) * P],
-                    rhs=v_words[a][:, cols].bitcast(FP8X4),
-                    rhs_scale=v_sc[PLANE_ROW[a] : P, cols],
-                    start=(a == 0),
-                    stop=(a == 2),
-                )
+        def pick_words(picked, table):
+            nc.vector.tensor_copy(picked[:].bitcast(U32), table[:].bitcast(U32).indirect(offs_sb[:]))
+            return picked
 
-        def new_banks():
-            return [[psum.tile([P, BANK], F32, name="acc", tag="acc") for hf in range(2)] for t in range(PACK)]
-
-        banks0 = new_banks()
-        st = stage_tile()
-        cast("scalar", st, raw_w1[0, 0][:], 0, 128)
-        raw_w2b = load_rows("w1_20b", 24, w1[1024:1536, 256:512])
-        quantize(w1q[0, 0], st, 0, 512)
-        pick_words(2)
-        raw_w1[0, 1] = load_rows("w1_01", 0, w1[0:512, 512:1024])
-        st = stage_tile()
-        cast("scalar", st, raw_w1[1, 0][:, :, 0:256], 0, 64)
-        cast("vector", st, raw_w1[1, 0][:, :, 256:512], 64, 128)
-        raw_w1[1, 1] = load_rows("w1_11", 16, w1[512:1024, 512:1024])
-        st2 = big(40, [P, 2048], BF16, "stage_w1_20")
-        cast("scalar", st2, raw_w2a[:], 0, 64)
-        quantize(w1q[1, 0], st, 0, 512)
-        cast("scalar", st2, raw_w2b[:, :, 0:128], 64, 96)
-        cast("vector", st2, raw_w2b[:, :, 128:256], 96, 128)
-        raw_w1[2, 1] = load_rows("w1_21", 24, w1[1024:1536, 512:1024])
-        raw_w3 = [load_rows("w3_0", 8, w3[0:512, :])]
-        for t in range(PACK):
-            quantize(w1q[2, 0], st2, t * P, (t + 1) * P)
-            for a in range(3):
-                h_pass(banks0, a, 0, t)
-
-        w4_sb = big(40, [P, 2 * 2 * N], U8, "w4_sb")
-        w4_sc = big(42, [P, 2 * N], U8, "w4_sc")
-        nc.vector.tensor_copy(
-            out=w4_sb[:].bitcast(U16).rearrange("p (a t q) -> p a q t", a=2, t=PACK),
-            in_=w4_raw[:].bitcast(U16).rearrange("p (a q t) -> p a q t", a=2, t=PACK),
-        )
-        nc.vector.tensor_copy(
-            out=w4_sc[:].rearrange("p (a t q) -> p a q t", a=2, t=PACK),
-            in_=w4s_raw[:].rearrange("p (a q t) -> p a q t", a=2, t=PACK),
-        )
-
-        def evacuate(banks, b, t):
-            h = ring.tile([P, S], F32, name="h", tag="h", bufs=6)
-            for hf in range(2):
-                dst = h[:, hf * BANK : (hf + 1) * BANK]
-                nc.scalar.activation(out=dst, in_=banks[t][hf][:], func=ACT.Identity, bias=b1_sb[:, b, t : t + 1])
-            return h
-
-        def pick2(h, b, t):
-            g = big(32 + 2 * t, [P, M], F32, "g2_%d%d" % (b, t))
-            nc.vector.tensor_copy(g[:], h[:].indirect(pos2_sb[:]))
-            return g
-
-        def tanh(g):
-            th = ring.tile([P, M], F32, name="th", tag="th", bufs=6)
-            nc.scalar.activation(out=th[:], in_=g[:], func=ACT.Tanh)
-            return th
-
-        def pick1(d, h, th, m0, w):
-            nc.vector.tensor_tensor(d, h[:].indirect(pos1_sb[:, m0 // 16 : (m0 + w) // 16]), th[:, m0 : m0 + w], ALU.subtract)
-
-        def scale_round(stage, d, b, w):
-            nc.vector.tensor_tensor(
-                out=stage[:, 0 : PACK * w].rearrange("p (c i t) -> p c t i", i=4, t=PACK),
-                in0=d[:].rearrange("p t (c i) -> p c t i", i=4),
-                in1=gain_sb[:, b, :].unsqueeze(1).unsqueeze(3).to_broadcast([P, w // 4, PACK, 4]),
-                op=ALU.mult,
+        v_words = [pick_words(placed("v_words0", 32, [P, S], I32), tab0)]
+        w1_raw10 = load_pass("w1_raw10", 36, w1[PASS : 2 * PASS, 0:PASS])
+        w1_raw20_low = load_pass("w1_raw20_low", 44, w1[2 * PASS : K, 0 : PASS // 2])
+        w1_raw20_high = load_pass("w1_raw20_high", 48, w1[2 * PASS : K, PASS // 2 : PASS])
+        v_words.append(pick_words(keep.tile([P, S], I32, name="v_words1", align_bytes=64), tab1))
+        w4_sc_raw = placed("w4_sc_raw", 8, [P, 2 * N], U8)
+        w4_sc_raw32 = w4_sc_raw[:].bitcast(I32)
+        nc.vector.memset(w4_sc_raw32, 0)
+        for i in range(4):
+            nc.sync.dma_start(
+                out=w4_sc_raw32[i:P:32, :].rearrange("p (b w) -> p b w", b=2),
+                in_=w4_scales.bitcast(I32)[:, i:16:4, :].rearrange("b d w -> d b w"),
             )
 
-        d0 = keep.tile([P, PACK, M], F32, name="d0")
-        h = [None] * PACK
-        g = [None] * PACK
-        th = [None] * PACK
-        h[0] = evacuate(banks0, 0, 0)
-        g[0] = pick2(h[0], 0, 0)
-        for t in range(PACK):
-            if t + 1 < PACK:
-                h[t + 1] = evacuate(banks0, 0, t + 1)
-                g[t + 1] = pick2(h[t + 1], 0, t + 1)
-            if t == PACK - 1:
-                stw = [big(32, [P, 2048], BF16, "stage_w1_01")]
-                cast("scalar", stw[0], raw_w1[0, 1][:], 0, 128)
-                raw_w3.append(load_rows("w3_1", 0, w3[512:1024, :]))
-            th[t] = tanh(g[t])
-            pick1(d0[:, t, :], h[t], th[t], 0, M)
+        w1q = {}
 
-        banks1 = new_banks()
-        quantize(w1q[0, 1], stw[0], 0, 512)
-        st = stage_tile()
-        cast("scalar", st, raw_w1[1, 1][:], 0, 128)
-        quantize(w1q[1, 1], st, 0, 512)
-        st = stage_tile()
-        cast("scalar", st, raw_w1[2, 1][:], 0, 128)
-        stz = stage_tile()
-        scale_round(stz, d0, 0, M)
-        for t in range(PACK):
-            quantize(w1q[2, 1], st, t * P, (t + 1) * P)
+        def quantize_w1(a, b, rounded, slices, tiles):
+            quantize(tiles, 0, rounded[:, slices[0] * PASS : (slices[-1] + 1) * PASS])
+            for t in slices:
+                w1q[a, b, t] = (tiles[0], tiles[1], (t - slices[0]) * P)
+
+        def late_tiles(b, kib):
+            return placed("late_words%d" % b, kib, [P, 2 * P], I32), placed("late_scales%d" % b, kib + 1, [P, 2 * P], U8)
+
+        def h_products(b, t):
+            banks = [psum.tile([P, BANK], F32, name="acc", tag="acc") for half in range(S // BANK)]
             for a in range(3):
-                h_pass(banks1, a, 1, t)
-        quantize(zq[0], stz, 0, 512)
-        st = stage_tile()
-        cast("scalar", st, raw_w3[0][:, :, 0:256], 0, 64)
-        cast("vector", st, raw_w3[0][:, :, 256:512], 64, 128)
+                words, scales, c0 = w1q[a, b, t]
+                for half, bank in enumerate(banks):
+                    cols = slice(half * BANK, (half + 1) * BANK)
+                    nc.tensor.matmul_mx(
+                        out=bank[:],
+                        lhsT=words[:, c0 : c0 + P].bitcast(FP8X4),
+                        lhsT_scale=scales[:, c0 : c0 + P],
+                        rhs=v_words[a][:, cols].bitcast(FP8X4),
+                        rhs_scale=v_sc[PLANE_ROW[a] : P, cols],
+                        start=(a == 0),
+                        stop=(a == 2),
+                    )
+            return banks
 
-        h[0] = evacuate(banks1, 1, 0)
-        g[0] = pick2(h[0], 1, 0)
-        quantize(w3q[0], st, 0, 512)
+        def last_pass(b, rounded1, rounded2, late_kib):
+            banks = []
+            for t in range(PACK):
+                if t == 2:
+                    quantize_w1(1, b, rounded1, (2, 3), late_tiles(b, late_kib))
+                quantize_w1(2, b, rounded2, (t,), mx_tiles("w1q2%d%d" % (b, t), P))
+                banks.append(h_products(b, t))
+            return banks
+
+        def rounded_tile():
+            return ring.tile([P, PACK * PASS], BF16, name="rounded", tag="rounded", bufs=2, align_bytes=64)
+
+        rounded00 = rounded_tile()
+        round_weight(nc.scalar, rounded00, w1_raw00[:], 0)
+        quantize_w1(0, 0, rounded00, (0, 1, 2, 3), mx_tiles("w1q00", PASS))
+        v_words.append(pick_words(placed("v_words2", 16, [P, S], I32), tab2))
+        w1_raw01 = load_pass("w1_raw01", 24, w1[0:PASS, PASS:H])
+        rounded10 = rounded_tile()
+        round_in_halves(rounded10, w1_raw10)
+        w1_raw11 = load_pass("w1_raw11", 36, w1[PASS : 2 * PASS, PASS:H])
+        rounded20 = placed("rounded20", 56, [P, PACK * PASS], BF16)
+        round_weight(nc.scalar, rounded20, w1_raw20_low[:], 0)
+        quantize_w1(1, 0, rounded10, (0, 1), mx_tiles("w1q10", 2 * P))
+        round_weight(nc.scalar, rounded20, w1_raw20_high[:, :, 0 : PASS // 4], P // 2)
+        round_weight(nc.vector, rounded20, w1_raw20_high[:, :, PASS // 4 : PASS // 2], 3 * P // 4)
+        banks = last_pass(0, rounded10, rounded20, 48)
+
+        w4_sc = placed("w4_sc", 56, [P, 2 * N], U8)
+        nc.vector.tensor_copy(
+            out=w4_sc[:].rearrange("p (b t q) -> p b q t", b=2, t=PACK),
+            in_=w4_sc_raw[:].rearrange("p (b q t) -> p b q t", b=2, t=PACK),
+        )
+        w3_raw0 = load_pass("w3_raw0", 59, w3[0:PASS, :])
+        w1_raw21 = load_pass("w1_raw21", 44, w1[2 * PASS : K, PASS:H])
+
+        def h_slice(b, t, pair):
+            h = ring.tile([P, S], F32, name="h", tag="h", bufs=6)
+            for half, bank in enumerate(pair):
+                nc.scalar.activation(
+                    out=h[:, half * BANK : (half + 1) * BANK], in_=bank[:], func=ACT.Identity, bias=b1_sb[:, b, t : t + 1]
+                )
+            second = placed("second%d%d" % (b, t), 2 * t, [P, M], F32)
+            nc.vector.tensor_copy(second[:], h[:].indirect(pos2_sb[:]))
+            return h, second
+
+        def tanh(second):
+            bounded = ring.tile([P, M], F32, name="bounded", tag="bounded", bufs=6)
+            nc.scalar.activation(out=bounded[:], in_=second[:], func=ACT.Tanh)
+            return bounded
+
+        def difference(diff, h, bounded, m0):
+            width = diff.shape[1]
+            window = h[:].indirect(pos1_sb[:, m0 // 16 : (m0 + width) // 16])
+            nc.vector.tensor_tensor(diff, window, bounded[:, m0 : m0 + width], ALU.subtract)
+
+        def times_gain(b, diff):
+            width = diff.shape[2]
+            z = rounded_tile()[:, 0 : PACK * width]
+            factor = gain_sb[:, b, :].unsqueeze(1).unsqueeze(3).to_broadcast([P, width // LINE, PACK, LINE])
+            nc.vector.tensor_tensor(out=interleaved(z), in0=by_slice(diff[:]), in1=factor, op=ALU.mult)
+            return z
+
+        zq = [mx_tiles("zq%d" % b, M) for b in range(2)]
+        diff0 = keep.tile([P, PACK, M], F32, name="diff0")
+        slices = [h_slice(0, 0, banks[0])]
         for t in range(PACK):
             if t + 1 < PACK:
-                h[t + 1] = evacuate(banks1, 1, t + 1)
-                g[t + 1] = pick2(h[t + 1], 1, t + 1)
-            th[t] = tanh(g[t])
-        st = stage_tile()
-        cast("scalar", st, raw_w3[1][:], 0, 128)
-        nc.scalar.activation(out=warm[:], in_=th[PACK - 1][:, 0:1], func=ACT.Abs_reciprocal_sqrt, bias=2.0)
+                slices.append(h_slice(0, t + 1, banks[t + 1]))
+            else:
+                rounded01 = placed("rounded01", 0, [P, PACK * PASS], BF16)
+                round_weight(nc.scalar, rounded01, w1_raw01[:], 0)
+                w3_raw1 = load_pass("w3_raw1", 24, w3[PASS:H, :])
+            difference(diff0[:, t, :], slices[t][0], tanh(slices[t][1]), 0)
+        quantize_w1(0, 1, rounded01, (0, 1, 2, 3), mx_tiles("w1q01", PASS))
+        rounded11 = placed("rounded11", 4, [P, PACK * PASS], BF16)
+        round_weight(nc.scalar, rounded11, w1_raw11[:], 0)
+        quantize_w1(1, 1, rounded11, (0, 1), mx_tiles("w1q11", 2 * P))
+        rounded21 = placed("rounded21", 36, [P, PACK * PASS], BF16)
+        round_weight(nc.scalar, rounded21, w1_raw21[:], 0)
+        z0 = times_gain(0, diff0)
+        banks = last_pass(1, rounded11, rounded21, 48)
+        quantize(zq[0], 0, z0)
+        w3q = [mx_tiles("w3q%d" % b, N) for b in range(2)]
+        w3_rounded0 = placed("w3_rounded0", 44, [P, PACK * PASS], BF16)
+        round_in_halves(w3_rounded0, w3_raw0)
 
-        y_view = out_0.rearrange("(p t) m -> p t m", t=PACK)
-        words_view = out_1[0].rearrange("p m t -> p (m t)").bitcast(I32)
-
-        def products(m0):
+        slices = [h_slice(1, 0, banks[0])]
+        quantize(w3q[0], 0, w3_rounded0[:])
+        bounded1 = []
+        for t in range(PACK):
+            if t + 1 < PACK:
+                slices.append(h_slice(1, t + 1, banks[t + 1]))
+            bounded1.append(tanh(slices[t][1]))
+        w3_rounded1 = placed("w3_rounded1", 4, [P, PACK * PASS], BF16)
+        round_in_halves(w3_rounded1, w3_raw1)
+        def product(m0, stationary):
+            bank = psum.tile([P, PACK, BLOCK], F32, name="acc", tag="acc")
             cols = slice(m0, m0 + BLOCK)
-            extent = psum.tile([P, PACK, BLOCK], F32, name="acc", tag="acc")
-            change = psum.tile([P, PACK, BLOCK], F32, name="acc", tag="acc")
             for t in range(PACK):
                 for b in range(2):
+                    words, scales = stationary(b, t)
                     nc.tensor.matmul_mx(
-                        out=extent[:, t, :],
-                        lhsT=w3q[b][0][:, t * P : (t + 1) * P].bitcast(FP8X4),
-                        lhsT_scale=w3q[b][1][:, t * P : (t + 1) * P],
+                        out=bank[:, t, :],
+                        lhsT=words,
+                        lhsT_scale=scales,
                         rhs=zq[b][0][:, cols].bitcast(FP8X4),
                         rhs_scale=zq[b][1][:, cols],
                         start=(b == 0),
                         stop=(b == 1),
                     )
-            for t in range(PACK):
-                for b in range(2):
-                    c0 = b * N + t * P
-                    nc.tensor.matmul_mx(
-                        out=change[:, t, :],
-                        lhsT=w4_sb[:, 2 * c0 : 2 * (c0 + P)].bitcast(FP4X4),
-                        lhsT_scale=w4_sc[:, c0 : c0 + P],
-                        rhs=zq[b][0][:, cols].bitcast(FP8X4),
-                        rhs_scale=zq[b][1][:, cols],
-                        start=(b == 0),
-                        stop=(b == 1),
-                    )
-            return extent, change
+            return bank[:].rearrange("p t m -> p (t m)")
+
+        def w3_slice(b, t):
+            return w3q[b][0][:, t * P : (t + 1) * P].bitcast(FP8X4), w3q[b][1][:, t * P : (t + 1) * P]
+
+        def w4_slice(b, t):
+            c0 = b * N + t * P
+            return w4_sb[:, 2 * c0 : 2 * (c0 + P)].bitcast(FP4X4), w4_sc[:, c0 : c0 + P]
 
         def damping(extent):
-            a = ring.tile([P, BANK], F32, name="absx", tag="absx", bufs=2)
-            r = ring.tile([P, BANK], F32, name="root", tag="root", bufs=2)
-            r2 = ring.tile([P, BANK], F32, name="recip", tag="recip", bufs=2)
-            nc.scalar.activation(out=a[:], in_=extent[:].rearrange("p t m -> p (t m)"), func=ACT.Abs)
-            nc.scalar.activation(out=r[:], in_=a[:], func=ACT.Abs_reciprocal_sqrt, bias=1.0)
-            nc.scalar.activation(out=r2[:], in_=r[:], func=ACT.Square)
-            return r2
+            halves = [slice(i * BANK // 2, (i + 1) * BANK // 2) for i in range(2)]
+            size = [ring.tile([P, BANK // 2], F32, name="size", tag="size%d" % i, bufs=1) for i in range(2)]
+            root = [ring.tile([P, BANK // 2], F32, name="root", tag="root%d" % i, bufs=1) for i in range(2)]
+            factor = ring.tile([P, BANK], F32, name="damp", tag="damp", bufs=M // BLOCK)
+            for i, cols in enumerate(halves):
+                nc.scalar.activation(out=size[i][:], in_=extent[:, cols], func=ACT.Abs)
+            for i in range(2):
+                nc.scalar.activation(out=root[i][:], in_=size[i][:], func=ACT.Abs_reciprocal_sqrt, bias=1.0)
+            for i, cols in enumerate(halves):
+                nc.scalar.activation(out=factor[:, cols], in_=root[i][:], func=ACT.Square)
+            return factor
 
-        def finish(change, r2, m0):
-            y = ring.tile([P, PACK, BLOCK], F32, name="y", tag="y", bufs=4)
-            yb = ring.tile([P, PACK * BLOCK], BF16, name="yb", tag="yb", bufs=2, align_bytes=64)
-            nc.vector.tensor_tensor(
-                out=y[:].rearrange("p t m -> p (t m)"), in0=change[:].rearrange("p t m -> p (t m)"), in1=r2[:], op=ALU.mult
-            )
-            nc.sync.dma_start(out=y_view[:, :, m0 : m0 + BLOCK], in_=y[:])
-            nc.vector.tensor_copy(
-                out=yb[:].rearrange("p (c i t) -> p c t i", i=4, t=PACK), in_=y[:].rearrange("p t (c i) -> p c t i", i=4)
-            )
-            quantize((y_words, y_sc), yb, m0, m0 + BLOCK, base=m0)
-            nc.sync.dma_start(out=words_view[:, m0 : m0 + BLOCK], in_=y_words[:, m0 : m0 + BLOCK])
-
-        pending = []
-        for m0, w in CHUNKS:
-            d = keep.tile([P, PACK, w], F32, name="d1_%d" % m0)
+        products = []
+        for c in range(M // BLOCK):
+            m0 = c * BLOCK
+            diff = placed("diff1_%d" % c, 2 * ((c + 1) % PACK), [P, PACK, BLOCK], F32)
             for t in range(PACK):
-                pick1(d[:, t, :], h[t], th[t], m0, w)
-            if m0 == 0:
-                quantize(w3q[1], st, 0, 512)
-            stz = stage_tile()
-            scale_round(stz, d, 1, w)
-            quantize(zq[1], stz, m0, m0 + w, base=m0)
-            for mb in range(m0, m0 + w, BLOCK):
-                extent, change = products(mb)
-                pending.append((change, damping(extent), mb))
-        for change, r2, mb in pending:
-            finish(change, r2, mb)
+                difference(diff[:, t, :], slices[t][0], bounded1[t], m0)
+            if c == 0:
+                quantize(w3q[1], 0, w3_rounded1[:])
+            quantize(zq[1], m0, times_gain(1, diff))
+            extent = product(m0, w3_slice)
+            change = product(m0, w4_slice)
+            products.append((change, damping(extent)))
 
-        y_sc32 = y_sc[:].bitcast(I32)
-        sc_view = out_2[0].bitcast(I32)
-        for q in range(4):
-            eng = nc.sync if q % 2 == 0 else nc.scalar
-            eng.dma_start(out=sc_view[4 * q : 4 * q + 4, :], in_=y_sc32[32 * q : 32 * q + 4, :])
+        yq = mx_tiles("yq", M)
+        y_rows = out_0.rearrange("(p t) m -> p t m", t=PACK)
+        word_rows = out_1[0].rearrange("p m t -> p (m t)").bitcast(I32)
+        for c, (change, factor) in enumerate(products):
+            cols = slice(c * BLOCK, (c + 1) * BLOCK)
+            y = ring.tile([P, PACK, BLOCK], F32, name="y", tag="y", bufs=M // BLOCK)
+            y_rounded = ring.tile([P, PACK * BLOCK], BF16, name="y_rounded", tag="y_rounded", bufs=M // BLOCK, align_bytes=64)
+            nc.vector.tensor_tensor(out=y[:].rearrange("p t m -> p (t m)"), in0=change, in1=factor[:], op=ALU.mult)
+            nc.sync.dma_start(out=y_rows[:, :, cols], in_=y[:])
+            nc.vector.tensor_copy(out=interleaved(y_rounded[:]), in_=by_slice(y[:]))
+            quantize(yq, c * BLOCK, y_rounded[:])
+            nc.sync.dma_start(out=word_rows[:, cols], in_=yq[0][:, cols])
+
+        for d in range(4):
+            queue = nc.sync if d % 2 == 0 else nc.scalar
+            queue.dma_start(out=out_2[0].bitcast(I32)[4 * d : 4 * d + 4, :], in_=yq[1][:].bitcast(I32)[32 * d : 32 * d + 4, :])

from contextlib import ExitStack

import concourse.mybir as mybir

T, S, M, K, H, N = 2048, 1024, 512, 1536, 1024, 512
FLOPS = 2 * K * H * S + 2 * 2 * H * N * M

F32 = mybir.dt.float32
BF16 = mybir.dt.bfloat16
I32 = mybir.dt.int32
U32 = mybir.dt.uint32
U16 = mybir.dt.uint16
U8 = mybir.dt.uint8
FP8X4 = mybir.dt.float8_e4m3fn_x4
FP4X4 = mybir.dt.float4_e2m1fn_x4
ACT = mybir.ActivationFunctionType
ALU = mybir.AluOpType

P = 128
PACK = 4
PASS = P * PACK
BANK = 512
BLOCK = 128
LINE = 4
PLANE_ROW = (0, 8, 4)


def tile_list_song_theme_features_kernel(
    tc, tab_words, tab_scales, offs, pos1, pos2, w1, b1, gain, w4_words, w4_scales, w3, out_0, out_1, out_2
):
    nc = tc.nc
    with ExitStack() as ctx:
        keep = ctx.enter_context(tc.tile_pool(name="keep", bufs=1))
        ring = ctx.enter_context(tc.tile_pool(name="ring", bufs=1))
        shared = ctx.enter_context(tc.tile_pool(name="shared", bufs=1))
        psum = ctx.enter_context(tc.psum_pool(name="psum", bufs=8))

        def placed(name, kib, shape, dtype):
            return shared.tile(shape, dtype, name=name, offset=1024 * kib, align_bytes=64)

        def mx_tiles(name, width):
            words = keep.tile([P, width], I32, name=name + "_words", align_bytes=64)
            scales = keep.tile([P, width], U8, name=name + "_scales", align_bytes=64)
            return words, scales

        def load_pass(name, kib, rows):
            raw = placed(name, kib, [P, PACK, rows.shape[1]], F32)
            nc.sync.dma_start(out=raw[:], in_=rows.rearrange("(p j) c -> p j c", j=PACK))
            return raw

        def load_table(a, kib):
            words = placed("tab%d" % a, kib, [P, T], I32)
            nc.sync.dma_start(out=words[:], in_=tab_words[a].rearrange("p t i -> p (t i)").bitcast(I32))
            return words

        def round_weight(engine, rounded, raw, q0):
            count = raw.shape[2] // PACK
            dst = rounded[:].rearrange("p (t q j) -> p q j t", t=PACK, j=PACK)[:, q0 : q0 + count]
            src = raw.rearrange("p j (q t) -> p q j t", t=PACK)
            if engine is nc.scalar:
                nc.scalar.activation(out=dst, in_=src, func=ACT.Copy)
            else:
                nc.vector.tensor_copy(out=dst, in_=src)

        def round_in_halves(rounded, raw):
            round_weight(nc.scalar, rounded, raw[:, :, 0 : PASS // 2], 0)
            round_weight(nc.vector, rounded, raw[:, :, PASS // 2 : PASS], P // 2)

        def quantize(tiles, c0, values):
            cols = slice(c0, c0 + values.shape[1] // PACK)
            nc.vector.quantize_mx(out=tiles[0][:, cols].bitcast(FP8X4), scales=tiles[1][:, cols], in_=values)

        def interleaved(tile):
            return tile.rearrange("p (c i t) -> p c t i", i=LINE, t=PACK)

        def by_slice(tile):
            return tile.rearrange("p t (c i) -> p c t i", i=LINE)

        offs_sb = keep.tile([P, S // 16], U16, name="offs_sb")
        pos1_sb = keep.tile([P, M // 16], U16, name="pos1_sb")
        pos2_sb = keep.tile([P, M // 16], U16, name="pos2_sb")
        b1_sb = keep.tile([P, 2, PACK], F32, name="b1_sb")
        gain_sb = keep.tile([P, 2, PACK], F32, name="gain_sb")

        tab_sc = placed("tab_sc", 31, [P, T], U8)
        tab_sc32 = tab_sc[:].bitcast(I32)
        nc.vector.memset(tab_sc32, 0)
        w4_raw = placed("w4_raw", 15, [P, 2 * 2 * N], U8)
        nc.sync.dma_start(
            out=w4_raw[:].bitcast(I32).rearrange("p (b w) -> p b w", b=2), in_=w4_words.bitcast(I32).rearrange("b p w -> p b w")
        )
        nc.sync.dma_start(offs_sb[:], offs)
        nc.sync.dma_start(pos2_sb[:], pos2)
        nc.sync.dma_start(pos1_sb[:], pos1)
        tab0 = load_table(0, 43)
        rows32 = tab_scales.bitcast(I32)
        for e in range(2):
            nc.sync.dma_start(out=tab_sc32[e:P:8, :], in_=rows32[0:2, e:16:2, :].rearrange("a g w -> g a w"))
            nc.sync.dma_start(out=tab_sc32[PLANE_ROW[2] + e : P : 16, :], in_=rows32[2, e:16:2, :])
        nc.gpsimd.dma_start(out=b1_sb[:], in_=b1.rearrange("(b p t) -> p b t", b=2, t=PACK))
        nc.gpsimd.dma_start(out=gain_sb[:], in_=gain.rearrange("(b p t) -> p b t", b=2, t=PACK))

        w4_sb = keep.tile([P, 2 * 2 * N], U8, name="w4_sb", align_bytes=64)
        nc.vector.tensor_copy(
            out=w4_sb[:].bitcast(U16).rearrange("p (b t q) -> p b q t", b=2, t=PACK),
            in_=w4_raw[:].bitcast(U16).rearrange("p (b q t) -> p b q t", b=2, t=PACK),
        )
        tab1 = load_table(1, 8)
        w1_raw00 = load_pass("w1_raw00", 16, w1[0:PASS, 0:PASS])

        picked_sc = keep.tile([P, S], U8, name="picked_sc", align_bytes=64)
        nc.vector.tensor_copy(picked_sc[:], tab_sc[:].indirect(offs_sb[:]))
        tab2 = load_table(2, 24)
        v_sc = keep.tile([P, S], U8, name="v_sc", align_bytes=64)
        v_sc32 = v_sc[:].bitcast(I32)
        nc.vector.tensor_copy(out=v_sc32, in_=picked_sc[:].bitcast(I32))
        for e in range(2):
            nc.sync.dma_start(out=v_sc32[2 + e : P - 14 + e : 4, :], in_=v_sc32[16 + e : P : 4, :])

        def pick_words(picked, table):
            nc.vector.tensor_copy(picked[:].bitcast(U32), table[:].bitcast(U32).indirect(offs_sb[:]))
            return picked

        v_words = [pick_words(placed("v_words0", 32, [P, S], I32), tab0)]
        w1_raw10 = load_pass("w1_raw10", 36, w1[PASS : 2 * PASS, 0:PASS])
        w1_raw20_low = load_pass("w1_raw20_low", 44, w1[2 * PASS : K, 0 : PASS // 2])
        w1_raw20_high = load_pass("w1_raw20_high", 48, w1[2 * PASS : K, PASS // 2 : PASS])
        v_words.append(pick_words(keep.tile([P, S], I32, name="v_words1", align_bytes=64), tab1))
        w4_sc_raw = placed("w4_sc_raw", 8, [P, 2 * N], U8)
        w4_sc_raw32 = w4_sc_raw[:].bitcast(I32)
        nc.vector.memset(w4_sc_raw32, 0)
        for i in range(4):
            nc.sync.dma_start(
                out=w4_sc_raw32[i:P:32, :].rearrange("p (b w) -> p b w", b=2),
                in_=w4_scales.bitcast(I32)[:, i:16:4, :].rearrange("b d w -> d b w"),
            )

        w1q = {}

        def quantize_w1(a, b, rounded, slices, tiles):
            quantize(tiles, 0, rounded[:, slices[0] * PASS : (slices[-1] + 1) * PASS])
            for t in slices:
                w1q[a, b, t] = (tiles[0], tiles[1], (t - slices[0]) * P)

        def late_tiles(b, kib):
            return placed("late_words%d" % b, kib, [P, 2 * P], I32), placed("late_scales%d" % b, kib + 1, [P, 2 * P], U8)

        def h_products(b, t):
            banks = [psum.tile([P, BANK], F32, name="acc", tag="acc") for half in range(S // BANK)]
            for a in range(3):
                words, scales, c0 = w1q[a, b, t]
                for half, bank in enumerate(banks):
                    cols = slice(half * BANK, (half + 1) * BANK)
                    nc.tensor.matmul_mx(
                        out=bank[:],
                        lhsT=words[:, c0 : c0 + P].bitcast(FP8X4),
                        lhsT_scale=scales[:, c0 : c0 + P],
                        rhs=v_words[a][:, cols].bitcast(FP8X4),
                        rhs_scale=v_sc[PLANE_ROW[a] : P, cols],
                        start=(a == 0),
                        stop=(a == 2),
                    )
            return banks

        def last_pass(b, rounded1, rounded2, late_kib):
            banks = []
            for t in range(PACK):
                if t == 2:
                    quantize_w1(1, b, rounded1, (2, 3), late_tiles(b, late_kib))
                quantize_w1(2, b, rounded2, (t,), mx_tiles("w1q2%d%d" % (b, t), P))
                banks.append(h_products(b, t))
            return banks

        def rounded_tile():
            return ring.tile([P, PACK * PASS], BF16, name="rounded", tag="rounded", bufs=2, align_bytes=64)

        rounded00 = rounded_tile()
        round_weight(nc.scalar, rounded00, w1_raw00[:], 0)
        quantize_w1(0, 0, rounded00, (0, 1, 2, 3), mx_tiles("w1q00", PASS))
        v_words.append(pick_words(placed("v_words2", 16, [P, S], I32), tab2))
        w1_raw01 = load_pass("w1_raw01", 24, w1[0:PASS, PASS:H])
        rounded10 = rounded_tile()
        round_in_halves(rounded10, w1_raw10)
        w1_raw11 = load_pass("w1_raw11", 36, w1[PASS : 2 * PASS, PASS:H])
        rounded20 = placed("rounded20", 56, [P, PACK * PASS], BF16)
        round_weight(nc.scalar, rounded20, w1_raw20_low[:], 0)
        quantize_w1(1, 0, rounded10, (0, 1), mx_tiles("w1q10", 2 * P))
        round_weight(nc.scalar, rounded20, w1_raw20_high[:, :, 0 : PASS // 4], P // 2)
        round_weight(nc.vector, rounded20, w1_raw20_high[:, :, PASS // 4 : PASS // 2], 3 * P // 4)
        banks = last_pass(0, rounded10, rounded20, 48)

        w4_sc = placed("w4_sc", 56, [P, 2 * N], U8)
        nc.vector.tensor_copy(
            out=w4_sc[:].rearrange("p (b t q) -> p b q t", b=2, t=PACK),
            in_=w4_sc_raw[:].rearrange("p (b q t) -> p b q t", b=2, t=PACK),
        )
        w3_raw0 = load_pass("w3_raw0", 59, w3[0:PASS, :])
        w1_raw21 = load_pass("w1_raw21", 44, w1[2 * PASS : K, PASS:H])

        def h_slice(b, t, pair):
            h = ring.tile([P, S], F32, name="h", tag="h", bufs=6)
            for half, bank in enumerate(pair):
                nc.scalar.activation(
                    out=h[:, half * BANK : (half + 1) * BANK], in_=bank[:], func=ACT.Identity, bias=b1_sb[:, b, t : t + 1]
                )
            second = placed("second%d%d" % (b, t), 2 * t, [P, M], F32)
            nc.vector.tensor_copy(second[:], h[:].indirect(pos2_sb[:]))
            return h, second

        def tanh(second):
            bounded = ring.tile([P, M], F32, name="bounded", tag="bounded", bufs=6)
            nc.scalar.activation(out=bounded[:], in_=second[:], func=ACT.Tanh)
            return bounded

        def difference(diff, h, bounded, m0):
            width = diff.shape[1]
            window = h[:].indirect(pos1_sb[:, m0 // 16 : (m0 + width) // 16])
            nc.vector.tensor_tensor(diff, window, bounded[:, m0 : m0 + width], ALU.subtract)

        def times_gain(b, diff):
            width = diff.shape[2]
            z = rounded_tile()[:, 0 : PACK * width]
            factor = gain_sb[:, b, :].unsqueeze(1).unsqueeze(3).to_broadcast([P, width // LINE, PACK, LINE])
            nc.vector.tensor_tensor(out=interleaved(z), in0=by_slice(diff[:]), in1=factor, op=ALU.mult)
            return z

        zq = [mx_tiles("zq%d" % b, M) for b in range(2)]
        diff0 = keep.tile([P, PACK, M], F32, name="diff0")
        slices = [h_slice(0, 0, banks[0])]
        for t in range(PACK):
            if t + 1 < PACK:
                slices.append(h_slice(0, t + 1, banks[t + 1]))
            else:
                rounded01 = placed("rounded01", 0, [P, PACK * PASS], BF16)
                round_weight(nc.scalar, rounded01, w1_raw01[:], 0)
                w3_raw1 = load_pass("w3_raw1", 24, w3[PASS:H, :])
            difference(diff0[:, t, :], slices[t][0], tanh(slices[t][1]), 0)
        quantize_w1(0, 1, rounded01, (0, 1, 2, 3), mx_tiles("w1q01", PASS))
        rounded11 = placed("rounded11", 4, [P, PACK * PASS], BF16)
        round_weight(nc.scalar, rounded11, w1_raw11[:], 0)
        quantize_w1(1, 1, rounded11, (0, 1), mx_tiles("w1q11", 2 * P))
        rounded21 = placed("rounded21", 36, [P, PACK * PASS], BF16)
        round_weight(nc.scalar, rounded21, w1_raw21[:], 0)
        z0 = times_gain(0, diff0)
        banks = last_pass(1, rounded11, rounded21, 48)
        quantize(zq[0], 0, z0)
        w3q = [mx_tiles("w3q%d" % b, N) for b in range(2)]
        w3_rounded0 = placed("w3_rounded0", 44, [P, PACK * PASS], BF16)
        round_in_halves(w3_rounded0, w3_raw0)

        slices = [h_slice(1, 0, banks[0])]
        quantize(w3q[0], 0, w3_rounded0[:])
        bounded1 = []
        for t in range(PACK):
            if t + 1 < PACK:
                slices.append(h_slice(1, t + 1, banks[t + 1]))
            bounded1.append(tanh(slices[t][1]))
        w3_rounded1 = placed("w3_rounded1", 4, [P, PACK * PASS], BF16)
        round_in_halves(w3_rounded1, w3_raw1)
        def product(m0, stationary):
            bank = psum.tile([P, PACK, BLOCK], F32, name="acc", tag="acc")
            cols = slice(m0, m0 + BLOCK)
            for t in range(PACK):
                for b in range(2):
                    words, scales = stationary(b, t)
                    nc.tensor.matmul_mx(
                        out=bank[:, t, :],
                        lhsT=words,
                        lhsT_scale=scales,
                        rhs=zq[b][0][:, cols].bitcast(FP8X4),
                        rhs_scale=zq[b][1][:, cols],
                        start=(b == 0),
                        stop=(b == 1),
                    )
            return bank[:].rearrange("p t m -> p (t m)")

        def w3_slice(b, t):
            return w3q[b][0][:, t * P : (t + 1) * P].bitcast(FP8X4), w3q[b][1][:, t * P : (t + 1) * P]

        def w4_slice(b, t):
            c0 = b * N + t * P
            return w4_sb[:, 2 * c0 : 2 * (c0 + P)].bitcast(FP4X4), w4_sc[:, c0 : c0 + P]

        def damping(extent):
            halves = [slice(i * BANK // 2, (i + 1) * BANK // 2) for i in range(2)]
            size = [ring.tile([P, BANK // 2], F32, name="size", tag="size%d" % i, bufs=1) for i in range(2)]
            root = [ring.tile([P, BANK // 2], F32, name="root", tag="root%d" % i, bufs=1) for i in range(2)]
            factor = ring.tile([P, BANK], F32, name="damp", tag="damp", bufs=M // BLOCK)
            for i, cols in enumerate(halves):
                nc.scalar.activation(out=size[i][:], in_=extent[:, cols], func=ACT.Abs)
            for i in range(2):
                nc.scalar.activation(out=root[i][:], in_=size[i][:], func=ACT.Abs_reciprocal_sqrt, bias=1.0)
            for i, cols in enumerate(halves):
                nc.scalar.activation(out=factor[:, cols], in_=root[i][:], func=ACT.Square)
            return factor

        products = []
        for c in range(M // BLOCK):
            m0 = c * BLOCK
            diff = placed("diff1_%d" % c, 2 * ((c + 1) % PACK), [P, PACK, BLOCK], F32)
            for t in range(PACK):
                difference(diff[:, t, :], slices[t][0], bounded1[t], m0)
            if c == 0:
                quantize(w3q[1], 0, w3_rounded1[:])
            quantize(zq[1], m0, times_gain(1, diff))
            extent = product(m0, w3_slice)
            change = product(m0, w4_slice)
            products.append((change, damping(extent)))

        yq = mx_tiles("yq", M)
        y_rows = out_0.rearrange("(p t) m -> p t m", t=PACK)
        word_rows = out_1[0].rearrange("p m t -> p (m t)").bitcast(I32)
        for c, (change, factor) in enumerate(products):
            cols = slice(c * BLOCK, (c + 1) * BLOCK)
            y = ring.tile([P, PACK, BLOCK], F32, name="y", tag="y", bufs=M // BLOCK)
            y_rounded = ring.tile([P, PACK * BLOCK], BF16, name="y_rounded", tag="y_rounded", bufs=M // BLOCK, align_bytes=64)
            nc.vector.tensor_tensor(out=y[:].rearrange("p t m -> p (t m)"), in0=change, in1=factor[:], op=ALU.mult)
            nc.sync.dma_start(out=y_rows[:, :, cols], in_=y[:])
            nc.vector.tensor_copy(out=interleaved(y_rounded[:]), in_=by_slice(y[:]))
            quantize(yq, c * BLOCK, y_rounded[:])
            nc.sync.dma_start(out=word_rows[:, cols], in_=yq[0][:, cols])

        for d in range(4):
            queue = nc.sync if d % 2 == 0 else nc.scalar
            queue.dma_start(out=out_2[0].bitcast(I32)[4 * d : 4 * d + 4, :], in_=yq[1][:].bitcast(I32)[32 * d : 32 * d + 4, :])
